import numpy as np
import ml_dtypes


def mxq(x, axis, fmt="e4m3"):
    dtype, down = {"e4m3": (ml_dtypes.float8_e4m3fn, 7), "e5m2": (ml_dtypes.float8_e5m2, 14)}[fmt]
    v = np.moveaxis(np.asarray(x, np.float32).astype(ml_dtypes.bfloat16).astype(np.float64), axis, -1)
    blocks = v.reshape(v.shape[:-1] + (-1, 32))
    amax = np.abs(blocks).max(-1, keepdims=True)
    byte = np.maximum(np.where(amax > 0, np.frexp(amax)[1] - 1 + 127, 0) - down, 1)
    scale = np.exp2(byte - 127.0)
    codes = (blocks / scale).astype(np.float32).astype(dtype).astype(np.float64)
    return np.moveaxis((codes * scale).reshape(v.shape), -1, axis)


WIDE = False


def mx_kscale(k):
    if not WIDE:
        return np.ones(k)
    levels = np.array([30, -30])
    if k % 512:
        return np.exp2(np.random.permutation(np.resize(levels, k // 32))).repeat(32)
    a = np.empty((k // 512, 16))
    for p in range(k // 512):
        a[p, :8] = np.random.permutation(np.resize(levels, 8))
        for g in range(8):
            far = levels[np.abs(levels - a[p, g]) >= 10]
            a[p, g + 8] = far[np.random.randint(len(far))]
    return np.exp2(a.ravel()).repeat(32)


def f64(x):
    return np.asarray(x).astype(np.float64)


def striped(idx):
    return np.tile(np.asarray(idx).reshape(-1, 16).T, (8, 1)).astype(np.uint16)


def unstriped(offs):
    return offs[:16].T.reshape(-1).astype(np.int64)


E2M1 = np.array([0.0, 0.5, 1.0, 1.5, 2.0, 3.0, 4.0, 6.0, -0.0, -0.5, -1.0, -1.5, -2.0, -3.0, -4.0, -6.0])


def pack_weight(w, fmt):
    k, n = w.shape
    w = f64(np.asarray(w, np.float32).astype(ml_dtypes.bfloat16)).reshape(k // 32, 32, n)
    amax = np.abs(w).max(1)
    if fmt in ("e4m3", "e5m2"):
        byte = np.frexp(amax)[1] - 1 + 127 - (7 if fmt == "e4m3" else 14)
    else:
        mant, ex = np.frexp(amax / 6.0)
        byte = np.where(mant > 0.5, ex, ex - 1) + 127
    byte = np.clip(np.where(amax > 0, byte, 1), 1, 254)
    scaled = (w * np.exp2(127.0 - byte)[:, None, :]).reshape(k, n).astype(np.float32)
    by_word = np.ascontiguousarray(scaled.reshape(k // 512, 128, 4, n).transpose(0, 1, 3, 2))
    if fmt in ("e4m3", "e5m2"):
        words = by_word.astype(ml_dtypes.float8_e4m3fn if fmt == "e4m3" else ml_dtypes.float8_e5m2).view(np.uint8)
    else:
        c = by_word.astype(ml_dtypes.float4_e2m1fn).view(np.uint8) & 0xF
        words = (c[..., 0::2] | (c[..., 1::2] << 4)).reshape(k // 512, 128, 2 * n)
    return np.ascontiguousarray(words), np.ascontiguousarray(byte.astype(np.uint8).reshape(k // 512, 16, n))


def unpack_weight(words, scales, fmt):
    g, _, n = scales.shape
    words = np.ascontiguousarray(words).reshape(g, 128, n, -1)
    if fmt in ("e4m3", "e5m2"):
        vals = words.view(ml_dtypes.float8_e4m3fn if fmt == "e4m3" else ml_dtypes.float8_e5m2).astype(np.float64)
    else:
        nib = np.empty((g, 128, n, 4), np.uint8)
        nib[..., 0::2] = words & 0xF
        nib[..., 1::2] = words >> 4
        vals = E2M1[nib]
    vals = vals * np.repeat(np.exp2(scales.astype(np.float64) - 127.0), 8, axis=1)[..., None]
    return vals.transpose(0, 1, 3, 2).reshape(g * 512, n)


def sgn(shape):
    return np.random.uniform(0.5, 2.0, shape) * np.where(np.random.standard_normal(shape) < 0, -1.0, 1.0)


K, T, J, R, C, I, O, N = 512, 1024, 256, 512, 256, 128, 128, 256


def setup_inputs():
    n = np.random.standard_normal
    idx = np.random.permutation(T)[:J]
    idx2 = np.random.permutation(J)[:I]
    idx3 = np.random.permutation(J)[:I]
    idx4 = np.random.permutation(C)[:I]
    idx5 = np.random.permutation(C)[:O]
    fk = mx_kscale(K)
    fr = mx_kscale(R)
    xtp = pack_weight(n((K, T)) / fk[:, None], "e4m3")
    wp = pack_weight(n((K, R)) * 1 / np.sqrt(K) * fk[:, None], "e2m1")
    w2p = pack_weight(n((K, R)) * 1 / np.sqrt(K) * fk[:, None], "e5m2")
    wbp = pack_weight(n((R, N)) * 1 / np.sqrt(R) / fr[:, None], "e5m2")
    return {
        "xt_words": xtp[0],
        "xt_scales": xtp[1],
        "w_words": wp[0],
        "w_scales": wp[1],
        "w2_words": w2p[0],
        "w2_scales": w2p[1],
        "sa": (sgn((R, 1))).astype(np.float32),
        "sb": (np.random.uniform(0.5, 1.6, (R, 1)) * fr[:, None]).astype(np.float32),
        "wb_words": wbp[0],
        "wb_scales": wbp[1],
        "offs": striped(idx),
        "offs2": striped(idx2),
        "offs3": striped(idx3),
        "offs4": striped(idx4),
        "offs5": striped(idx5),
    }


def reference(xt_words, xt_scales, w_words, w_scales, w2_words, w2_scales, sa, sb, wb_words, wb_scales, offs, offs2, offs3, offs4, offs5):
    idx = unstriped(offs)
    idx2 = unstriped(offs2)
    idx3 = unstriped(offs3)
    idx4 = unstriped(offs4)
    idx5 = unstriped(offs5)
    xtu = unpack_weight(xt_words, xt_scales, "e4m3")
    wu = unpack_weight(w_words, w_scales, "e2m1")
    w2u = unpack_weight(w2_words, w2_scales, "e5m2")
    wbu = unpack_weight(wb_words, wb_scales, "e5m2")
    xtidxg = xtu[:, idx]
    a = wu.T @ xtidxg
    b = w2u.T @ xtidxg
    h1 = np.maximum(a[:, idx2] * f64(sa), b[:, idx3])
    pw = np.zeros((R, C))
    pw[:, idx4] = h1 * f64(sb)
    hid = pw[:, idx5]
    hidq = mxq(hid, 0, "e4m3")
    p = wbu.T @ hidq
    return p

@@ -1,0 +1,166 @@
+import concourse.mybir as mybir
+
+F32 = mybir.dt.float32
+BF16 = mybir.dt.bfloat16
+I32 = mybir.dt.int32
+U32 = mybir.dt.uint32
+U16 = mybir.dt.uint16
+U8 = mybir.dt.uint8
+E4M3 = mybir.dt.float8_e4m3fn_x4
+E5M2 = mybir.dt.float8_e5m2_x4
+E2M1 = mybir.dt.float4_e2m1fn_x4
+COPY = mybir.ActivationFunctionType.Copy
+MAX = mybir.AluOpType.max
+
+K, T, J, R, C, I, O, N = 512, 1024, 256, 512, 256, 128, 128, 256
+P = 128
+PACK = 4
+QUADS = 4
+FLOPS = 2 * K * R * J * 2 + 2 * R * N * O
+
+
+def tile_list_seatsput_kernel(
+    tc, xt_words, xt_scales, w_words, w_scales, w2_words, w2_scales, sa, sb, wb_words, wb_scales,
+    offs, offs2, offs3, offs4, offs5, out,
+):
+    nc = tc.nc
+    with (
+        tc.tile_pool(name="held", bufs=1) as held,
+        tc.psum_pool(name="psum", bufs=1) as psum,
+    ):
+        def words(dram):
+            return dram[0].rearrange("p n t -> p (n t)").bitcast(I32)
+
+        def load_list(dram, n, name):
+            tile = held.tile([P, n // 16], U16, name=name)
+            nc.sync.dma_start(tile[:], dram)
+            return tile
+
+        def zero_plane(cols, name):
+            plane = held.tile([P, cols], U8, name=name, align_bytes=64)
+            nc.vector.memset(plane[:].bitcast(I32), 0)
+            return plane
+
+        def load_rows_direct(plane, dram):
+            for q in range(QUADS):
+                nc.sync.dma_start(plane[32 * q : 32 * q + 4, :].bitcast(I32), dram[0, 4 * q : 4 * q + 4, :].bitcast(I32))
+
+        def load_rows_staged(dram, name):
+            staged = held.tile([4, QUADS, R // 4], I32, name=name)
+            nc.sync.dma_start(staged[:], dram[0].bitcast(I32).rearrange("(q r) n -> r q n", r=4))
+            return staged
+
+        def spread_and_deal(staged, plane, name):
+            for q in range(QUADS):
+                nc.vector.tensor_copy(plane[32 * q : 32 * q + 4, :].bitcast(I32), staged[:, q, :])
+            dealt = held.tile([P, PACK, P], U8, name=name, align_bytes=64)
+            nc.vector.tensor_copy(dealt[:], plane[:].rearrange("p (m t) -> p t m", t=PACK))
+            return dealt
+
+        xs_plane = zero_plane(T, "xs_plane")
+        ws_plane = zero_plane(R, "ws_plane")
+        w2s_plane = zero_plane(R, "w2s_plane")
+        wbs_plane = zero_plane(N, "wbs_plane")
+        pages = [held.tile([P, C], F32, name=f"page{t}") for t in range(PACK)]
+        for page in pages:
+            nc.vector.memset(page[:], 0.0)
+
+        ws_staged = load_rows_staged(w_scales, "ws_staged")
+        w_raw = held.tile([P, 2 * R], U8, name="w_raw")
+        nc.scalar.dma_start(w_raw[:].bitcast(I32), w_words[0].bitcast(I32))
+        load_rows_direct(xs_plane, xt_scales)
+        idx = load_list(offs, J, "idx")
+        x_raw = held.tile([P, T], U32, name="x_raw")
+        nc.sync.dma_start(x_raw[:].bitcast(I32), words(xt_words))
+        w2s_staged = load_rows_staged(w2_scales, "w2s_staged")
+        w2_raw = held.tile([P, R], U32, name="w2_raw")
+        nc.sync.dma_start(w2_raw[:].bitcast(I32), words(w2_words))
+        idx2 = load_list(offs2, I, "idx2")
+        sa_sb = held.tile([P, PACK], F32, name="sa_sb")
+        nc.sync.dma_start(sa_sb[:], sa.rearrange("(p t) o -> p (t o)", t=PACK))
+        idx3 = load_list(offs3, I, "idx3")
+        idx4 = load_list(offs4, I, "idx4")
+        sb_sb = held.tile([P, PACK], F32, name="sb_sb")
+        nc.sync.dma_start(sb_sb[:], sb.rearrange("(p t) o -> p (t o)", t=PACK))
+        idx5 = load_list(offs5, O, "idx5")
+        wb_raw = held.tile([P, N], U32, name="wb_raw", align_bytes=64)
+        nc.sync.dma_start(wb_raw[:].bitcast(I32), words(wb_words))
+        load_rows_direct(wbs_plane, wb_scales)
+
+        ws = spread_and_deal(ws_staged, ws_plane, "ws")
+        w = held.tile([P, PACK, 2 * P], U8, name="w", align_bytes=64)
+        nc.scalar.copy(w[:].bitcast(U16), w_raw[:].bitcast(U16).rearrange("p (m t) -> p t m", t=PACK))
+
+        xg = held.tile([P, J], U32, name="xg", align_bytes=64)
+        nc.vector.tensor_copy(xg[:], x_raw[:].indirect(idx[:]))
+        xgs = held.tile([P, J], U8, name="xgs", align_bytes=64)
+        nc.vector.tensor_copy(xgs[:], xs_plane[:].indirect(idx[:]))
+
+        w2s = spread_and_deal(w2s_staged, w2s_plane, "w2s")
+        w2 = held.tile([P, PACK, P], U32, name="w2", align_bytes=64)
+        nc.scalar.copy(
+            w2[:].rearrange("p t (c i) -> p c t i", i=4),
+            w2_raw[:].rearrange("p (c i t) -> p c t i", i=4, t=PACK),
+        )
+
+        def first_stage(lhsT, lhsT_scale, name, copy_out):
+            acc = psum.tile([P, J], F32, name=name + "_acc")
+            nc.tensor.matmul_mx(
+                out=acc[:], lhsT=lhsT, lhsT_scale=lhsT_scale, rhs=xg[:].bitcast(E4M3), rhs_scale=xgs[:],
+                start=True, stop=True,
+            )
+            rows = held.tile([P, J], F32, name=name)
+            copy_out(rows[:], acc[:])
+            return rows
+
+        pairs = [held.tile([P, 2, I], F32, name=f"pair{t}", tag=f"pair{t}", align_bytes=64) for t in range(PACK)]
+        h1 = [held.tile([P, I], F32, name=f"h1_{t}") for t in range(PACK)]
+
+        def seat_a(t):
+            copy_out = nc.scalar.copy if t < 2 else nc.vector.tensor_copy
+            a = first_stage(w[:, t, :].bitcast(E2M1), ws[:, t, :], f"a{t}", copy_out)
+            nc.scalar.activation(pairs[t][:, 0, :], a[:].indirect(idx2[:]), COPY, scale=sa_sb[:, t : t + 1])
+
+        def seat_b(t):
+            b = first_stage(w2[:, t, :].bitcast(E5M2), w2s[:, t, :], f"b{t}", nc.vector.tensor_copy)
+            nc.vector.tensor_copy(pairs[t][:, 1, :], b[:].indirect(idx3[:]))
+
+        def larger(t):
+            nc.vector.tensor_tensor(h1[t][:], pairs[t][:, 0, :], pairs[t][:, 1, :], MAX)
+
+        def put(t):
+            nc.scalar.activation(pages[t][:].indirect(idx4[:]), h1[t][:], COPY, scale=sb_sb[:, t : t + 1])
+
+        seat_a(0)
+        seat_b(0)
+        larger(0)
+        for t in range(1, PACK):
+            seat_a(t)
+        put(0)
+        for t in range(1, PACK):
+            seat_b(t)
+            larger(t)
+            put(t)
+
+        hid = held.tile([P, PACK * O], BF16, name="hid", tag=f"pair{PACK - 1}", align_bytes=64)
+        for t in range(PACK):
+            nc.scalar.activation(hid[:, t : PACK * O : PACK], pages[t][:].indirect(idx5[:]), COPY)
+
+        hq = held.tile([P, O], U32, name="hq", align_bytes=64)
+        hqs = held.tile([P, O], U8, name="hqs", align_bytes=64)
+        nc.vector.quantize_mx(out=hq[:].bitcast(E4M3), scales=hqs[:], in_=hid[:])
+
+        for half in range(N // P):
+            cols = slice(half * P, (half + 1) * P)
+            acc = psum.tile([P, O], F32, name=f"a{half}_acc")
+            nc.tensor.matmul_mx(
+                out=acc[:], lhsT=wb_raw[:, cols].bitcast(E5M2), lhsT_scale=wbs_plane[:, cols],
+                rhs=hq[:].bitcast(E4M3), rhs_scale=hqs[:], start=True, stop=True,
+            )
+            result = held.tile([P, O], F32, name=f"result{half}")
+            if half == 0:
+                nc.vector.tensor_copy(result[:], acc[:])
+                nc.sync.dma_start(out[cols, :], result[:])
+            else:
+                nc.scalar.copy(result[:], acc[:])
+                nc.scalar.dma_start(out[cols, :], result[:])

@@ -47,7 +47,7 @@ def tile_list_seatsput_kernel(
 
         def load_rows_staged(dram, name):
             staged = held.tile([4, QUADS, R // 4], I32, name=name)
-            nc.sync.dma_start(staged[:], dram[0].bitcast(I32).rearrange("(q r) n -> r q n", r=4))
+            nc.scalar.dma_start(staged[:], dram[0].bitcast(I32).rearrange("(q r) n -> r q n", r=4))
             return staged
 
         def spread_and_deal(staged, plane, name):
@@ -66,13 +66,13 @@ def tile_list_seatsput_kernel(
             nc.vector.memset(page[:], 0.0)
 
         ws_staged = load_rows_staged(w_scales, "ws_staged")
-        w_raw = held.tile([P, 2 * R], U8, name="w_raw")
-        nc.scalar.dma_start(w_raw[:].bitcast(I32), w_words[0].bitcast(I32))
-        load_rows_direct(xs_plane, xt_scales)
+        w2s_staged = load_rows_staged(w2_scales, "w2s_staged")
         idx = load_list(offs, J, "idx")
         x_raw = held.tile([P, T], U32, name="x_raw")
         nc.sync.dma_start(x_raw[:].bitcast(I32), words(xt_words))
-        w2s_staged = load_rows_staged(w2_scales, "w2s_staged")
+        load_rows_direct(xs_plane, xt_scales)
+        w_raw = held.tile([P, 2 * R], U8, name="w_raw")
+        nc.sync.dma_start(w_raw[:].bitcast(I32), w_words[0].bitcast(I32))
         w2_raw = held.tile([P, R], U32, name="w2_raw")
         nc.sync.dma_start(w2_raw[:].bitcast(I32), words(w2_words))
         idx2 = load_list(offs2, I, "idx2")
@@ -88,6 +88,7 @@ def tile_list_seatsput_kernel(
         load_rows_direct(wbs_plane, wb_scales)
 
         ws = spread_and_deal(ws_staged, ws_plane, "ws")
+        w2s = spread_and_deal(w2s_staged, w2s_plane, "w2s")
         w = held.tile([P, PACK, 2 * P], U8, name="w", align_bytes=64)
         nc.scalar.copy(w[:].bitcast(U16), w_raw[:].bitcast(U16).rearrange("p (m t) -> p t m", t=PACK))
 
@@ -96,20 +97,19 @@ def tile_list_seatsput_kernel(
         xgs = held.tile([P, J], U8, name="xgs", align_bytes=64)
         nc.vector.tensor_copy(xgs[:], xs_plane[:].indirect(idx[:]))
 
-        w2s = spread_and_deal(w2s_staged, w2s_plane, "w2s")
         w2 = held.tile([P, PACK, P], U32, name="w2", align_bytes=64)
         nc.scalar.copy(
             w2[:].rearrange("p t (c i) -> p c t i", i=4),
             w2_raw[:].rearrange("p (c i t) -> p c t i", i=4, t=PACK),
         )
 
-        def first_stage(lhsT, lhsT_scale, name, copy_out):
-            acc = psum.tile([P, J], F32, name=name + "_acc")
+        def first_stage(lhsT, lhsT_scale, name, copy_out, tag, bank):
+            acc = psum.tile([P, J], F32, name=name + "_acc", tag=bank)
             nc.tensor.matmul_mx(
                 out=acc[:], lhsT=lhsT, lhsT_scale=lhsT_scale, rhs=xg[:].bitcast(E4M3), rhs_scale=xgs[:],
                 start=True, stop=True,
             )
-            rows = held.tile([P, J], F32, name=name)
+            rows = held.tile([P, J], F32, name=name, tag=tag)
             copy_out(rows[:], acc[:])
             return rows
 
@@ -117,12 +117,11 @@ def tile_list_seatsput_kernel(
         h1 = [held.tile([P, I], F32, name=f"h1_{t}") for t in range(PACK)]
 
         def seat_a(t):
-            copy_out = nc.scalar.copy if t < 2 else nc.vector.tensor_copy
-            a = first_stage(w[:, t, :].bitcast(E2M1), ws[:, t, :], f"a{t}", copy_out)
+            a = first_stage(w[:, t, :].bitcast(E2M1), ws[:, t, :], f"a{t}", nc.scalar.copy, f"a{t}", f"acc_a{t % 2}")
             nc.scalar.activation(pairs[t][:, 0, :], a[:].indirect(idx2[:]), COPY, scale=sa_sb[:, t : t + 1])
 
         def seat_b(t):
-            b = first_stage(w2[:, t, :].bitcast(E5M2), w2s[:, t, :], f"b{t}", nc.vector.tensor_copy)
+            b = first_stage(w2[:, t, :].bitcast(E5M2), w2s[:, t, :], f"b{t}", nc.vector.tensor_copy, f"b{t % 2}", f"acc_b{t % 2}")
             nc.vector.tensor_copy(pairs[t][:, 1, :], b[:].indirect(idx3[:]))
 
         def larger(t):
@@ -152,7 +151,7 @@ def tile_list_seatsput_kernel(
 
         for half in range(N // P):
             cols = slice(half * P, (half + 1) * P)
-            acc = psum.tile([P, O], F32, name=f"a{half}_acc")
+            acc = psum.tile([P, O], F32, name=f"out{half}_acc")
             nc.tensor.matmul_mx(
                 out=acc[:], lhsT=wb_raw[:, cols].bitcast(E5M2), lhsT_scale=wbs_plane[:, cols],
                 rhs=hq[:].bitcast(E4M3), rhs_scale=hqs[:], start=True, stop=True,

@@ -14,8 +14,11 @@ MAX = mybir.AluOpType.max
 
 K, T, J, R, C, I, O, N = 512, 1024, 256, 512, 256, 128, 128, 256
 P = 128
-PACK = 4
+SLOTS = 4
 QUADS = 4
+ROWS = 4
+EARLY = 2
+BANKS = 2
 FLOPS = 2 * K * R * J * 2 + 2 * R * N * O
 
 
@@ -26,105 +29,116 @@ def tile_list_seatsput_kernel(
     nc = tc.nc
     with (
         tc.tile_pool(name="held", bufs=1) as held,
+        tc.tile_pool(name="reused", bufs=1) as reused,
         tc.psum_pool(name="psum", bufs=1) as psum,
     ):
-        def words(dram):
-            return dram[0].rearrange("p n t -> p (n t)").bitcast(I32)
 
-        def load_list(dram, n, name):
-            tile = held.tile([P, n // 16], U16, name=name)
+        def load_words(tile, dram):
+            nc.sync.dma_start(tile[:].bitcast(I32), dram[0].rearrange("p n t -> p (n t)").bitcast(I32))
+
+        def load_list(dram, entries, name):
+            tile = held.tile([P, entries // 16], U16, name=name)
             nc.sync.dma_start(tile[:], dram)
             return tile
 
-        def zero_plane(cols, name):
-            plane = held.tile([P, cols], U8, name=name, align_bytes=64)
+        def load_per_row(dram, name):
+            tile = held.tile([P, SLOTS], F32, name=name)
+            nc.sync.dma_start(tile[:], dram.rearrange("(p t) o -> p (t o)", t=SLOTS))
+            return tile
+
+        def zero_plane(columns, name):
+            plane = held.tile([P, columns], U8, name=name, tag=name, align_bytes=64)
             nc.vector.memset(plane[:].bitcast(I32), 0)
             return plane
 
-        def load_rows_direct(plane, dram):
-            for q in range(QUADS):
-                nc.sync.dma_start(plane[32 * q : 32 * q + 4, :].bitcast(I32), dram[0, 4 * q : 4 * q + 4, :].bitcast(I32))
+        def load_scale_rows(plane, dram, quads):
+            for q in quads:
+                nc.sync.dma_start(
+                    plane[32 * q : 32 * q + ROWS, :].bitcast(I32), dram[0, ROWS * q : ROWS * (q + 1), :].bitcast(I32)
+                )
 
-        def load_rows_staged(dram, name):
-            staged = held.tile([4, QUADS, R // 4], I32, name=name)
-            nc.scalar.dma_start(staged[:], dram[0].bitcast(I32).rearrange("(q r) n -> r q n", r=4))
-            return staged
-
-        def spread_and_deal(staged, plane, name):
-            for q in range(QUADS):
-                nc.vector.tensor_copy(plane[32 * q : 32 * q + 4, :].bitcast(I32), staged[:, q, :])
-            dealt = held.tile([P, PACK, P], U8, name=name, align_bytes=64)
-            nc.vector.tensor_copy(dealt[:], plane[:].rearrange("p (m t) -> p t m", t=PACK))
-            return dealt
+        def deal_scales(dealt, plane, slots):
+            nc.vector.tensor_copy(dealt[:], plane[:].rearrange("p (m t) -> p t m", t=SLOTS)[:, slots, :])
+            return [dealt[:, s, :] for s in range(slots.stop - slots.start)]
 
         xs_plane = zero_plane(T, "xs_plane")
         ws_plane = zero_plane(R, "ws_plane")
         w2s_plane = zero_plane(R, "w2s_plane")
         wbs_plane = zero_plane(N, "wbs_plane")
-        pages = [held.tile([P, C], F32, name=f"page{t}") for t in range(PACK)]
+        pages = [held.tile([P, C], F32, name=f"page{t}") for t in range(SLOTS)]
         for page in pages:
             nc.vector.memset(page[:], 0.0)
 
-        ws_staged = load_rows_staged(w_scales, "ws_staged")
-        w2s_staged = load_rows_staged(w2_scales, "w2s_staged")
+        ws_staged = held.tile([ROWS, QUADS, R // 4], I32, name="ws_staged")
+        nc.scalar.dma_start(ws_staged[:], w_scales[0].bitcast(I32).rearrange("(q i) n -> i q n", i=ROWS))
         idx = load_list(offs, J, "idx")
-        x_raw = held.tile([P, T], U32, name="x_raw")
-        nc.sync.dma_start(x_raw[:].bitcast(I32), words(xt_words))
-        load_rows_direct(xs_plane, xt_scales)
-        w_raw = held.tile([P, 2 * R], U8, name="w_raw")
+        w_raw = held.tile([P, 2 * R], U8, name="w_raw", align_bytes=64)
         nc.sync.dma_start(w_raw[:].bitcast(I32), w_words[0].bitcast(I32))
-        w2_raw = held.tile([P, R], U32, name="w2_raw")
-        nc.sync.dma_start(w2_raw[:].bitcast(I32), words(w2_words))
+        load_scale_rows(xs_plane, xt_scales, range(QUADS))
+        x_raw = held.tile([P, T], U32, name="x_raw", align_bytes=64)
+        load_words(x_raw, xt_words)
+        w2_raw = reused.tile([P, R], U32, name="w2_raw", offset=0)
+        load_words(w2_raw, w2_words)
+        load_scale_rows(w2s_plane, w2_scales, range(QUADS))
         idx2 = load_list(offs2, I, "idx2")
-        sa_sb = held.tile([P, PACK], F32, name="sa_sb")
-        nc.sync.dma_start(sa_sb[:], sa.rearrange("(p t) o -> p (t o)", t=PACK))
+        sa_sb = load_per_row(sa, "sa_sb")
         idx3 = load_list(offs3, I, "idx3")
         idx4 = load_list(offs4, I, "idx4")
-        sb_sb = held.tile([P, PACK], F32, name="sb_sb")
-        nc.sync.dma_start(sb_sb[:], sb.rearrange("(p t) o -> p (t o)", t=PACK))
+        sb_sb = load_per_row(sb, "sb_sb")
         idx5 = load_list(offs5, O, "idx5")
         wb_raw = held.tile([P, N], U32, name="wb_raw", align_bytes=64)
-        nc.sync.dma_start(wb_raw[:].bitcast(I32), words(wb_words))
-        load_rows_direct(wbs_plane, wb_scales)
+        load_words(wb_raw, wb_words)
+        load_scale_rows(wbs_plane, wb_scales, range(QUADS))
 
-        ws = spread_and_deal(ws_staged, ws_plane, "ws")
-        w2s = spread_and_deal(w2s_staged, w2s_plane, "w2s")
-        w = held.tile([P, PACK, 2 * P], U8, name="w", align_bytes=64)
-        nc.scalar.copy(w[:].bitcast(U16), w_raw[:].bitcast(U16).rearrange("p (m t) -> p t m", t=PACK))
+        for q in range(QUADS):
+            nc.vector.tensor_copy(ws_plane[32 * q : 32 * q + ROWS, :].bitcast(I32), ws_staged[:, q, :])
+        early, late = slice(0, EARLY), slice(EARLY, SLOTS)
+        ws_early = held.tile([P, EARLY, P], U8, name="ws_early", align_bytes=64)
+        ws = deal_scales(ws_early, ws_plane, early)
+        w2s_early = held.tile([P, EARLY, P], U8, name="w2s_early", align_bytes=64)
+        w2s = deal_scales(w2s_early, w2s_plane, early)
 
         xg = held.tile([P, J], U32, name="xg", align_bytes=64)
         nc.vector.tensor_copy(xg[:], x_raw[:].indirect(idx[:]))
         xgs = held.tile([P, J], U8, name="xgs", align_bytes=64)
         nc.vector.tensor_copy(xgs[:], xs_plane[:].indirect(idx[:]))
 
-        w2 = held.tile([P, PACK, P], U32, name="w2", align_bytes=64)
+        w = held.tile([P, SLOTS, 2 * P], U8, name="w", align_bytes=64)
+        w2 = held.tile([P, SLOTS, P], U32, name="w2", align_bytes=64)
+        nc.scalar.copy(w[:].bitcast(U16), w_raw[:].bitcast(U16).rearrange("p (m t) -> p t m", t=SLOTS))
         nc.scalar.copy(
-            w2[:].rearrange("p t (c i) -> p c t i", i=4),
-            w2_raw[:].rearrange("p (c i t) -> p c t i", i=4, t=PACK),
+            w2[:].rearrange("p t (c i) -> p c t i", i=4), w2_raw[:].rearrange("p (c i t) -> p c t i", i=4, t=SLOTS)
         )
 
-        def first_stage(lhsT, lhsT_scale, name, copy_out, tag, bank):
-            acc = psum.tile([P, J], F32, name=name + "_acc", tag=bank)
+        w2s_late = held.tile([P, SLOTS - EARLY, P], U8, name="w2s_late", align_bytes=64)
+        w2s = w2s + deal_scales(w2s_late, w2s_plane, late)
+        ws_late = held.tile([P, SLOTS - EARLY, P], U8, name="ws_late", tag="w2s_plane", align_bytes=64)
+        ws = ws + deal_scales(ws_late, ws_plane, late)
+
+        def first_stage(weight_words, weight_scales, name, bank):
+            acc = psum.tile([P, J], F32, name=name, tag=bank)
             nc.tensor.matmul_mx(
-                out=acc[:], lhsT=lhsT, lhsT_scale=lhsT_scale, rhs=xg[:].bitcast(E4M3), rhs_scale=xgs[:],
+                out=acc[:], lhsT=weight_words, lhsT_scale=weight_scales, rhs=xg[:].bitcast(E4M3), rhs_scale=xgs[:],
                 start=True, stop=True,
             )
-            rows = held.tile([P, J], F32, name=name, tag=tag)
-            copy_out(rows[:], acc[:])
-            return rows
+            return acc
 
-        pairs = [held.tile([P, 2, I], F32, name=f"pair{t}", tag=f"pair{t}", align_bytes=64) for t in range(PACK)]
-        h1 = [held.tile([P, I], F32, name=f"h1_{t}") for t in range(PACK)]
+        pairs = [held.tile([P, 2, I], F32, name=f"pair{t}", tag=f"pair{t}", align_bytes=64) for t in range(SLOTS)]
+        h1 = [held.tile([P, I], F32, name=f"h1_{t}") for t in range(SLOTS)]
 
         def seat_a(t):
-            a = first_stage(w[:, t, :].bitcast(E2M1), ws[:, t, :], f"a{t}", nc.scalar.copy, f"a{t}", f"acc_a{t % 2}")
+            acc = first_stage(w[:, t, :].bitcast(E2M1), ws[t], f"a{t}_acc", f"bank_a{t % BANKS}")
+            a = reused.tile([P, J], F32, name=f"a{t}", offset=4 * J * (t % BANKS))
+            nc.scalar.copy(a[:], acc[:])
             nc.scalar.activation(pairs[t][:, 0, :], a[:].indirect(idx2[:]), COPY, scale=sa_sb[:, t : t + 1])
 
         def seat_b(t):
-            b = first_stage(w2[:, t, :].bitcast(E5M2), w2s[:, t, :], f"b{t}", nc.vector.tensor_copy, f"b{t % 2}", f"acc_b{t % 2}")
+            acc = first_stage(w2[:, t, :].bitcast(E5M2), w2s[t], f"b{t}_acc", f"bank_b{t % BANKS}")
+            b = held.tile([P, J], F32, name=f"b{t}", tag=f"b{t % BANKS}")
+            nc.vector.tensor_copy(b[:], acc[:])
             nc.vector.tensor_copy(pairs[t][:, 1, :], b[:].indirect(idx3[:]))
 
-        def larger(t):
+        def keep_larger(t):
             nc.vector.tensor_tensor(h1[t][:], pairs[t][:, 0, :], pairs[t][:, 1, :], MAX)
 
         def put(t):
@@ -132,34 +146,31 @@ def tile_list_seatsput_kernel(
 
         seat_a(0)
         seat_b(0)
-        larger(0)
-        for t in range(1, PACK):
+        keep_larger(0)
+        for t in range(1, SLOTS):
             seat_a(t)
         put(0)
-        for t in range(1, PACK):
+        for t in range(1, SLOTS):
             seat_b(t)
-            larger(t)
+            keep_larger(t)
             put(t)
 
-        hid = held.tile([P, PACK * O], BF16, name="hid", tag=f"pair{PACK - 1}", align_bytes=64)
-        for t in range(PACK):
-            nc.scalar.activation(hid[:, t : PACK * O : PACK], pages[t][:].indirect(idx5[:]), COPY)
+        hid = held.tile([P, SLOTS * O], BF16, name="hid", tag=f"pair{SLOTS - 1}", align_bytes=64)
+        for t in range(SLOTS):
+            nc.scalar.activation(hid[:, t : SLOTS * O : SLOTS], pages[t][:].indirect(idx5[:]), COPY)
 
         hq = held.tile([P, O], U32, name="hq", align_bytes=64)
         hqs = held.tile([P, O], U8, name="hqs", align_bytes=64)
         nc.vector.quantize_mx(out=hq[:].bitcast(E4M3), scales=hqs[:], in_=hid[:])
 
-        for half in range(N // P):
-            cols = slice(half * P, (half + 1) * P)
+        ways_out = ((nc.vector.tensor_copy, nc.sync), (nc.scalar.copy, nc.scalar))
+        for half, (copy_out, queue) in enumerate(ways_out):
+            n_half = slice(half * P, (half + 1) * P)
             acc = psum.tile([P, O], F32, name=f"out{half}_acc")
             nc.tensor.matmul_mx(
-                out=acc[:], lhsT=wb_raw[:, cols].bitcast(E5M2), lhsT_scale=wbs_plane[:, cols],
+                out=acc[:], lhsT=wb_raw[:, n_half].bitcast(E5M2), lhsT_scale=wbs_plane[:, n_half],
                 rhs=hq[:].bitcast(E4M3), rhs_scale=hqs[:], start=True, stop=True,
             )
             result = held.tile([P, O], F32, name=f"result{half}")
-            if half == 0:
-                nc.vector.tensor_copy(result[:], acc[:])
-                nc.sync.dma_start(out[cols, :], result[:])
-            else:
-                nc.scalar.copy(result[:], acc[:])
-                nc.scalar.dma_start(out[cols, :], result[:])
+            copy_out(result[:], acc[:])
+            queue.dma_start(out[n_half, :], result[:])

import concourse.mybir as mybir

F32 = mybir.dt.float32
BF16 = mybir.dt.bfloat16
I32 = mybir.dt.int32
U32 = mybir.dt.uint32
U16 = mybir.dt.uint16
U8 = mybir.dt.uint8
E4M3 = mybir.dt.float8_e4m3fn_x4
E5M2 = mybir.dt.float8_e5m2_x4
E2M1 = mybir.dt.float4_e2m1fn_x4
COPY = mybir.ActivationFunctionType.Copy
MAX = mybir.AluOpType.max

K, T, J, R, C, I, O, N = 512, 1024, 256, 512, 256, 128, 128, 256
P = 128
SLOTS = 4
QUADS = 4
ROWS = 4
EARLY = 2
BANKS = 2
FLOPS = 2 * K * R * J * 2 + 2 * R * N * O


def tile_list_seatsput_kernel(
    tc, xt_words, xt_scales, w_words, w_scales, w2_words, w2_scales, sa, sb, wb_words, wb_scales,
    offs, offs2, offs3, offs4, offs5, out,
):
    nc = tc.nc
    with (
        tc.tile_pool(name="held", bufs=1) as held,
        tc.tile_pool(name="reused", bufs=1) as reused,
        tc.psum_pool(name="psum", bufs=1) as psum,
    ):

        def load_words(tile, dram):
            nc.sync.dma_start(tile[:].bitcast(I32), dram[0].rearrange("p n t -> p (n t)").bitcast(I32))

        def load_list(dram, entries, name):
            tile = held.tile([P, entries // 16], U16, name=name)
            nc.sync.dma_start(tile[:], dram)
            return tile

        def load_per_row(dram, name):
            tile = held.tile([P, SLOTS], F32, name=name)
            nc.sync.dma_start(tile[:], dram.rearrange("(p t) o -> p (t o)", t=SLOTS))
            return tile

        def zero_plane(columns, name):
            plane = held.tile([P, columns], U8, name=name, tag=name, align_bytes=64)
            nc.vector.memset(plane[:].bitcast(I32), 0)
            return plane

        def load_scale_rows(plane, dram, quads):
            for q in quads:
                nc.sync.dma_start(
                    plane[32 * q : 32 * q + ROWS, :].bitcast(I32), dram[0, ROWS * q : ROWS * (q + 1), :].bitcast(I32)
                )

        def deal_scales(dealt, plane, slots):
            nc.vector.tensor_copy(dealt[:], plane[:].rearrange("p (m t) -> p t m", t=SLOTS)[:, slots, :])
            return [dealt[:, s, :] for s in range(slots.stop - slots.start)]

        xs_plane = zero_plane(T, "xs_plane")
        ws_plane = zero_plane(R, "ws_plane")
        w2s_plane = zero_plane(R, "w2s_plane")
        wbs_plane = zero_plane(N, "wbs_plane")
        pages = [held.tile([P, C], F32, name=f"page{t}") for t in range(SLOTS)]
        for page in pages:
            nc.vector.memset(page[:], 0.0)

        ws_staged = held.tile([ROWS, QUADS, R // 4], I32, name="ws_staged")
        nc.scalar.dma_start(ws_staged[:], w_scales[0].bitcast(I32).rearrange("(q i) n -> i q n", i=ROWS))
        idx = load_list(offs, J, "idx")
        w_raw = held.tile([P, 2 * R], U8, name="w_raw", align_bytes=64)
        nc.sync.dma_start(w_raw[:].bitcast(I32), w_words[0].bitcast(I32))
        load_scale_rows(xs_plane, xt_scales, range(QUADS))
        x_raw = held.tile([P, T], U32, name="x_raw", align_bytes=64)
        load_words(x_raw, xt_words)
        w2_raw = reused.tile([P, R], U32, name="w2_raw", offset=0)
        load_words(w2_raw, w2_words)
        load_scale_rows(w2s_plane, w2_scales, range(QUADS))
        idx2 = load_list(offs2, I, "idx2")
        sa_sb = load_per_row(sa, "sa_sb")
        idx3 = load_list(offs3, I, "idx3")
        idx4 = load_list(offs4, I, "idx4")
        sb_sb = load_per_row(sb, "sb_sb")
        idx5 = load_list(offs5, O, "idx5")
        wb_raw = held.tile([P, N], U32, name="wb_raw", align_bytes=64)
        load_words(wb_raw, wb_words)
        load_scale_rows(wbs_plane, wb_scales, range(QUADS))

        for q in range(QUADS):
            nc.vector.tensor_copy(ws_plane[32 * q : 32 * q + ROWS, :].bitcast(I32), ws_staged[:, q, :])
        early, late = slice(0, EARLY), slice(EARLY, SLOTS)
        ws_early = held.tile([P, EARLY, P], U8, name="ws_early", align_bytes=64)
        ws = deal_scales(ws_early, ws_plane, early)
        w2s_early = held.tile([P, EARLY, P], U8, name="w2s_early", align_bytes=64)
        w2s = deal_scales(w2s_early, w2s_plane, early)

        xg = held.tile([P, J], U32, name="xg", align_bytes=64)
        nc.vector.tensor_copy(xg[:], x_raw[:].indirect(idx[:]))
        xgs = held.tile([P, J], U8, name="xgs", align_bytes=64)
        nc.vector.tensor_copy(xgs[:], xs_plane[:].indirect(idx[:]))

        w = held.tile([P, SLOTS, 2 * P], U8, name="w", align_bytes=64)
        w2 = held.tile([P, SLOTS, P], U32, name="w2", align_bytes=64)
        nc.scalar.copy(w[:].bitcast(U16), w_raw[:].bitcast(U16).rearrange("p (m t) -> p t m", t=SLOTS))
        nc.scalar.copy(
            w2[:].rearrange("p t (c i) -> p c t i", i=4), w2_raw[:].rearrange("p (c i t) -> p c t i", i=4, t=SLOTS)
        )

        w2s_late = held.tile([P, SLOTS - EARLY, P], U8, name="w2s_late", align_bytes=64)
        w2s = w2s + deal_scales(w2s_late, w2s_plane, late)
        ws_late = held.tile([P, SLOTS - EARLY, P], U8, name="ws_late", tag="w2s_plane", align_bytes=64)
        ws = ws + deal_scales(ws_late, ws_plane, late)

        def first_stage(weight_words, weight_scales, name, bank):
            acc = psum.tile([P, J], F32, name=name, tag=bank)
            nc.tensor.matmul_mx(
                out=acc[:], lhsT=weight_words, lhsT_scale=weight_scales, rhs=xg[:].bitcast(E4M3), rhs_scale=xgs[:],
                start=True, stop=True,
            )
            return acc

        pairs = [held.tile([P, 2, I], F32, name=f"pair{t}", tag=f"pair{t}", align_bytes=64) for t in range(SLOTS)]
        h1 = [held.tile([P, I], F32, name=f"h1_{t}") for t in range(SLOTS)]

        def seat_a(t):
            acc = first_stage(w[:, t, :].bitcast(E2M1), ws[t], f"a{t}_acc", f"bank_a{t % BANKS}")
            a = reused.tile([P, J], F32, name=f"a{t}", offset=4 * J * (t % BANKS))
            nc.scalar.copy(a[:], acc[:])
            nc.scalar.activation(pairs[t][:, 0, :], a[:].indirect(idx2[:]), COPY, scale=sa_sb[:, t : t + 1])

        def seat_b(t):
            acc = first_stage(w2[:, t, :].bitcast(E5M2), w2s[t], f"b{t}_acc", f"bank_b{t % BANKS}")
            b = held.tile([P, J], F32, name=f"b{t}", tag=f"b{t % BANKS}")
            nc.vector.tensor_copy(b[:], acc[:])
            nc.vector.tensor_copy(pairs[t][:, 1, :], b[:].indirect(idx3[:]))

        def keep_larger(t):
            nc.vector.tensor_tensor(h1[t][:], pairs[t][:, 0, :], pairs[t][:, 1, :], MAX)

        def put(t):
            nc.scalar.activation(pages[t][:].indirect(idx4[:]), h1[t][:], COPY, scale=sb_sb[:, t : t + 1])

        seat_a(0)
        seat_b(0)
        keep_larger(0)
        for t in range(1, SLOTS):
            seat_a(t)
        put(0)
        for t in range(1, SLOTS):
            seat_b(t)
            keep_larger(t)
            put(t)

        hid = held.tile([P, SLOTS * O], BF16, name="hid", tag=f"pair{SLOTS - 1}", align_bytes=64)
        for t in range(SLOTS):
            nc.scalar.activation(hid[:, t : SLOTS * O : SLOTS], pages[t][:].indirect(idx5[:]), COPY)

        hq = held.tile([P, O], U32, name="hq", align_bytes=64)
        hqs = held.tile([P, O], U8, name="hqs", align_bytes=64)
        nc.vector.quantize_mx(out=hq[:].bitcast(E4M3), scales=hqs[:], in_=hid[:])

        ways_out = ((nc.vector.tensor_copy, nc.sync), (nc.scalar.copy, nc.scalar))
        for half, (copy_out, queue) in enumerate(ways_out):
            n_half = slice(half * P, (half + 1) * P)
            acc = psum.tile([P, O], F32, name=f"out{half}_acc")
            nc.tensor.matmul_mx(
                out=acc[:], lhsT=wb_raw[:, n_half].bitcast(E5M2), lhsT_scale=wbs_plane[:, n_half],
                rhs=hq[:].bitcast(E4M3), rhs_scale=hqs[:], start=True, stop=True,
            )
            result = held.tile([P, O], F32, name=f"result{half}")
            copy_out(result[:], acc[:])
            queue.dma_start(out[n_half, :], result[:])
